import numpy as np
import ml_dtypes


def mxq(x, axis, fmt="e4m3"):
    dtype, down = {"e4m3": (ml_dtypes.float8_e4m3fn, 7), "e5m2": (ml_dtypes.float8_e5m2, 14)}[fmt]
    v = np.moveaxis(np.asarray(x, np.float32).astype(ml_dtypes.bfloat16).astype(np.float64), axis, -1)
    blocks = v.reshape(v.shape[:-1] + (-1, 32))
    amax = np.abs(blocks).max(-1, keepdims=True)
    byte = np.maximum(np.where(amax > 0, np.frexp(amax)[1] - 1 + 127, 0) - down, 1)
    scale = np.exp2(byte - 127.0)
    codes = (blocks / scale).astype(np.float32).astype(dtype).astype(np.float64)
    return np.moveaxis((codes * scale).reshape(v.shape), -1, axis)


WIDE = False


def mx_kscale(k):
    if not WIDE:
        return np.ones(k)
    levels = np.array([30, -30])
    if k % 512:
        return np.exp2(np.random.permutation(np.resize(levels, k // 32))).repeat(32)
    a = np.empty((k // 512, 16))
    for p in range(k // 512):
        a[p, :8] = np.random.permutation(np.resize(levels, 8))
        for g in range(8):
            far = levels[np.abs(levels - a[p, g]) >= 10]
            a[p, g + 8] = far[np.random.randint(len(far))]
    return np.exp2(a.ravel()).repeat(32)


def f64(x):
    return np.asarray(x).astype(np.float64)


def striped(idx):
    return np.tile(np.asarray(idx).reshape(-1, 16).T, (8, 1)).astype(np.uint16)


def unstriped(offs):
    return offs[:16].T.reshape(-1).astype(np.int64)


E2M1 = np.array([0.0, 0.5, 1.0, 1.5, 2.0, 3.0, 4.0, 6.0, -0.0, -0.5, -1.0, -1.5, -2.0, -3.0, -4.0, -6.0])


def pack_weight(w, fmt):
    k, n = w.shape
    w = f64(np.asarray(w, np.float32).astype(ml_dtypes.bfloat16)).reshape(k // 32, 32, n)
    amax = np.abs(w).max(1)
    if fmt == "e4m3":
        byte = np.frexp(amax)[1] - 1 + 127 - 7
    else:
        mant, ex = np.frexp(amax / 6.0)
        byte = np.where(mant > 0.5, ex, ex - 1) + 127
    byte = np.clip(np.where(amax > 0, byte, 1), 1, 254)
    scaled = (w * np.exp2(127.0 - byte)[:, None, :]).reshape(k, n).astype(np.float32)
    by_word = np.ascontiguousarray(scaled.reshape(k // 512, 128, 4, n).transpose(0, 1, 3, 2))
    if fmt == "e4m3":
        words = by_word.astype(ml_dtypes.float8_e4m3fn).view(np.uint8)
    else:
        c = by_word.astype(ml_dtypes.float4_e2m1fn).view(np.uint8) & 0xF
        words = (c[..., 0::2] | (c[..., 1::2] << 4)).reshape(k // 512, 128, 2 * n)
    return np.ascontiguousarray(words), np.ascontiguousarray(byte.astype(np.uint8).reshape(k // 512, 16, n))


def unpack_weight(words, scales, fmt):
    g, _, n = scales.shape
    words = np.ascontiguousarray(words).reshape(g, 128, n, -1)
    if fmt == "e4m3":
        vals = words.view(ml_dtypes.float8_e4m3fn).astype(np.float64)
    else:
        nib = np.empty((g, 128, n, 4), np.uint8)
        nib[..., 0::2] = words & 0xF
        nib[..., 1::2] = words >> 4
        vals = E2M1[nib]
    vals = vals * np.repeat(np.exp2(scales.astype(np.float64) - 127.0), 8, axis=1)[..., None]
    return vals.transpose(0, 1, 3, 2).reshape(g * 512, n)


K, T, J, I, S, G = 1024, 1024, 256, 256, 512, 32


def setup_inputs():
    n = np.random.standard_normal
    idx = np.random.permutation(T)[:J]
    idx2 = np.random.permutation(S)[:J]
    fk = mx_kscale(K)
    kyp = pack_weight(n((K, I)) / fk[:, None], "e4m3")
    return {
        "xf": (n((K, T)) * 0.03).astype(np.float32),
        "xb": (n((K, S))).astype(np.float32),
        "fk": (np.random.uniform(0.5, 2.0, (K, 1)) * fk[:, None]).astype(np.float32),
        "ky_words": kyp[0],
        "ky_scales": kyp[1],
        "bi": (np.random.uniform(-0.7, 0.7, (1, I))).astype(np.float32),
        "offs": striped(idx),
        "offs2": striped(idx2),
    }


def reference(xf, xb, fk, ky_words, ky_scales, bi, offs, offs2):
    idx = unstriped(offs)
    idx2 = unstriped(offs2)
    kyu = unpack_weight(ky_words, ky_scales, "e4m3")
    u = f64(xf)[:, idx] * f64(xb)[:, idx2] * f64(fk)
    uq = mxq(u, 0, "e5m2")
    a0 = uq.T @ kyu
    a = a0 + f64(bi)
    g1 = a.reshape(J, G, I // G).mean(axis=2)
    g2 = np.repeat(g1, I // G, axis=1)
    y = (a - g2) * np.abs(a)
    return y

@@ -1,0 +1,158 @@
+from contextlib import ExitStack
+
+import concourse.mybir as mybir
+from concourse.masks import make_identity
+
+K, T, J, I, S = 1024, 1024, 256, 256, 512
+BUNDLE = 8
+FLOPS = 2 * K * J * I
+
+F32 = mybir.dt.float32
+BF16 = mybir.dt.bfloat16
+I32 = mybir.dt.int32
+U32 = mybir.dt.uint32
+U16 = mybir.dt.uint16
+U8 = mybir.dt.uint8
+E4M3X4 = mybir.dt.float8_e4m3fn_x4
+E5M2X4 = mybir.dt.float8_e5m2_x4
+ALU = mybir.AluOpType
+ACT = mybir.ActivationFunctionType
+
+P = 128
+PACK = 4
+K_PASS = P * PACK
+PASSES = K // K_PASS
+HALVES = J // P
+LIST_COLS = J // 16
+PLANE_ORDER = (2, 0, 1, 3)
+
+
+def tile_list_scores_products_given_centred_kernel(tc, xf, xb, fk, ky_words, ky_scales, bi, offs, offs2, out):
+    nc = tc.nc
+    with ExitStack() as ctx:
+        keep = ctx.enter_context(tc.tile_pool(name="keep", bufs=1))
+        psum = ctx.enter_context(tc.psum_pool(name="psum", bufs=1))
+
+        offs_t = keep.tile([P, LIST_COLS], U16, name="offs_t")
+        offs2_t = keep.tile([P, LIST_COLS], U16, name="offs2_t")
+        fk_t = keep.tile([P, PASSES, PACK], F32, name="fk_t")
+        bi_col = keep.tile([P, 2], F32, name="bi_col")
+        ident = keep.tile([P, P], F32, name="ident")
+        bias = keep.tile([P, I], F32, name="bias")
+        ky_sc = keep.tile([P, PASSES, I], U8, name="ky_sc", align_bytes=64)
+        ky_w = [keep.tile([P, I], U32, name="ky_w%d" % z, align_bytes=64) for z in range(PASSES)]
+        xb_t = [keep.tile([P, PACK * S], F32, name="xb%d" % z) for z in range(PASSES)]
+        xf_t = [[keep.tile([P, T], F32, name="xf%d%d" % (z, t)) for t in range(PACK)] for z in range(PASSES)]
+        gb = [[keep.tile([P, J], F32, name="gb%d%d" % (z, t)) for t in range(PACK)] for z in range(PASSES)]
+        prod = [[keep.tile([P, J], F32, name="prod%d%d" % (z, t)) for t in range(PACK)] for z in range(PASSES)]
+        grouped = [[keep.tile([P, P, PACK], BF16, name="grp%d%d" % (z, h), align_bytes=64) for h in range(HALVES)]
+                   for z in range(PASSES)]
+        u_w = [[keep.tile([P, P], U32, name="uw%d%d" % (z, h), align_bytes=64) for h in range(HALVES)]
+               for z in range(PASSES)]
+        u_sc = [[keep.tile([P, P], U8, name="us%d%d" % (z, h), align_bytes=64) for h in range(HALVES)]
+                for z in range(PASSES)]
+
+        def load_xb(z):
+            rows = xb[z * K_PASS:(z + 1) * K_PASS, :]
+            nc.sync.dma_start(xb_t[z][:], rows.rearrange("(p t) s -> p (t s)", t=PACK))
+
+        def load_xf(z, t):
+            rows = xf[z * K_PASS:(z + 1) * K_PASS, :]
+            nc.sync.dma_start(xf_t[z][t][:], rows.rearrange("(p t) c -> p t c", t=PACK)[:, t, :])
+
+        load_xb(0)
+        nc.sync.dma_start(offs2_t[:], offs2)
+        nc.sync.dma_start(offs_t[:], offs)
+        nc.scalar.dma_start(bi_col[:], bi.rearrange("o (p c) -> p (o c)", c=2))
+        nc.scalar.dma_start(fk_t[:], fk.rearrange("(z p t) o -> p z (t o)", z=PASSES, t=PACK))
+        make_identity(nc, ident[:])
+        nc.gpsimd.memset(ky_sc[:].bitcast(I32), 0)
+        for q in range(4):
+            nc.gpsimd.dma_start(ky_sc[32 * q:32 * q + 4, :, :].bitcast(I32),
+                                ky_scales[:, 4 * q:4 * q + 4, :].rearrange("z r c -> r z c").bitcast(I32))
+        load_xf(0, PLANE_ORDER[0])
+        load_xf(0, PLANE_ORDER[1])
+        load_xb(1)
+        load_xf(0, PLANE_ORDER[2])
+        load_xf(0, PLANE_ORDER[3])
+        for t in PLANE_ORDER:
+            load_xf(1, t)
+        for z in range(PASSES):
+            nc.sync.dma_start(ky_w[z][:].bitcast(I32), ky_words[z].rearrange("p c r -> p (c r)").bitcast(I32))
+
+        def gather_xb(z, t):
+            nc.scalar.activation(gb[z][t][:], xb_t[z][:, t * S:(t + 1) * S].indirect(offs2_t[:]), ACT.Copy)
+
+        def product(z, t, h=None):
+            if h is None:
+                nc.vector.tensor_tensor(prod[z][t][:], xf_t[z][t][:].indirect(offs_t[:]), gb[z][t][:], ALU.mult)
+            else:
+                cols = slice(h * P, (h + 1) * P)
+                nc.vector.tensor_tensor(prod[z][t][:, cols], xf_t[z][t][:].indirect(offs_t[:, 8 * h:8 * h + 8]),
+                                        gb[z][t][:, cols], ALU.mult)
+
+        def round_into(z, t):
+            for h in range(HALVES):
+                src = prod[z][t][:, h * P:(h + 1) * P]
+                if t < 2:
+                    nc.scalar.activation(grouped[z][h][:, :, t], src, ACT.Copy, scale=fk_t[:, z, t:t + 1])
+                else:
+                    nc.vector.tensor_scalar(grouped[z][h][:, :, t], src, fk_t[:, z, t:t + 1], None, ALU.mult)
+
+        def quantize(z):
+            for h in range(HALVES):
+                nc.vector.quantize_mx(out=u_w[z][h][:].bitcast(E5M2X4), scales=u_sc[z][h][:],
+                                      in_=grouped[z][h][:].rearrange("p j t -> p (j t)"))
+
+        spread = psum.tile([P, 2, P], F32, name="spread")
+        for c in range(2):
+            nc.tensor.transpose(spread[:, c, :], bi_col[:, c:c + 1].to_broadcast([P, P]), ident[:])
+        nc.scalar.activation(bias[:].rearrange("p (n c) -> p n c", c=2), spread[:].rearrange("p c n -> p n c"),
+                             ACT.Copy)
+        for t in PLANE_ORDER:
+            gather_xb(0, t)
+
+        for t in PLANE_ORDER[:2]:
+            product(0, t)
+            round_into(0, t)
+        for t in PLANE_ORDER:
+            gather_xb(1, t)
+        for t in PLANE_ORDER[2:]:
+            product(0, t)
+            round_into(0, t)
+        quantize(0)
+        for t in PLANE_ORDER[:3]:
+            product(1, t)
+            round_into(1, t)
+        for h in range(HALVES):
+            product(1, PLANE_ORDER[3], h)
+        round_into(1, PLANE_ORDER[3])
+        quantize(1)
+
+        acc = [psum.tile([P, I], F32, name="acc%d" % h) for h in range(HALVES)]
+        for z in range(PASSES):
+            for h in range(HALVES):
+                nc.tensor.matmul_mx(out=acc[h][:], lhsT=u_w[z][h][:].bitcast(E5M2X4), lhsT_scale=u_sc[z][h][:],
+                                    rhs=ky_w[z][:].bitcast(E4M3X4), rhs_scale=ky_sc[:, z, :],
+                                    start=(z == 0), stop=(z == PASSES - 1))
+
+        a = [keep.tile([P, I], F32, name="a%d" % h) for h in range(HALVES)]
+        mag = [keep.tile([P, I], F32, name="mag%d" % h) for h in range(HALVES)]
+        sums = [keep.tile([P, I // BUNDLE], F32, name="sums%d" % h) for h in range(HALVES)]
+        cen = [keep.tile([P, I], F32, name="cen%d" % h) for h in range(HALVES)]
+        res = [keep.tile([P, I], F32, name="res%d" % h) for h in range(HALVES)]
+        for h in range(HALVES):
+            nc.vector.tensor_tensor(a[h][:], acc[h][:], bias[:], ALU.add)
+            nc.scalar.activation(mag[h][:], a[h][:], ACT.Abs)
+        for h in range(HALVES):
+            nc.vector.tensor_reduce(sums[h][:], a[h][:].rearrange("p (g e) -> p g e", e=BUNDLE),
+                                    mybir.AxisListType.X, ALU.add)
+        for h in range(HALVES):
+            nc.vector.scalar_tensor_tensor(cen[h][:].rearrange("p (g e) -> p g e", e=BUNDLE),
+                                           sums[h][:].unsqueeze(2).to_broadcast([P, I // BUNDLE, BUNDLE]),
+                                           -1.0 / BUNDLE,
+                                           a[h][:].rearrange("p (g e) -> p g e", e=BUNDLE),
+                                           ALU.mult, ALU.add)
+        for h in range(HALVES):
+            nc.vector.tensor_tensor(res[h][:], cen[h][:], mag[h][:], ALU.mult)
+            nc.sync.dma_start(out[h * P:(h + 1) * P, :], res[h][:])

@@ -24,7 +24,6 @@ K_PASS = P * PACK
 PASSES = K // K_PASS
 HALVES = J // P
 LIST_COLS = J // 16
-PLANE_ORDER = (2, 0, 1, 3)
 
 
 def tile_list_scores_products_given_centred_kernel(tc, xf, xb, fk, ky_words, ky_scales, bi, offs, offs2, out):
@@ -42,97 +41,95 @@ def tile_list_scores_products_given_centred_kernel(tc, xf, xb, fk, ky_words, ky_
         ky_sc = keep.tile([P, PASSES, I], U8, name="ky_sc", align_bytes=64)
         ky_w = [keep.tile([P, I], U32, name="ky_w%d" % z, align_bytes=64) for z in range(PASSES)]
         xb_t = [keep.tile([P, PACK * S], F32, name="xb%d" % z) for z in range(PASSES)]
-        xf_t = [[keep.tile([P, T], F32, name="xf%d%d" % (z, t)) for t in range(PACK)] for z in range(PASSES)]
+        xf0 = keep.tile([P, PACK * T], F32, name="xf0")
+        xf1 = [keep.tile([P, T], F32, name="xf1%d" % t) for t in range(PACK)]
+        gf0 = [keep.tile([P, J], F32, name="gf0%d" % t) for t in range(PACK)]
+        prod0 = keep.tile([P, PACK, J], F32, name="prod0")
         gb = [[keep.tile([P, J], F32, name="gb%d%d" % (z, t)) for t in range(PACK)] for z in range(PASSES)]
-        prod = [[keep.tile([P, J], F32, name="prod%d%d" % (z, t)) for t in range(PACK)] for z in range(PASSES)]
-        grouped = [[keep.tile([P, P, PACK], BF16, name="grp%d%d" % (z, h), align_bytes=64) for h in range(HALVES)]
-                   for z in range(PASSES)]
-        u_w = [[keep.tile([P, P], U32, name="uw%d%d" % (z, h), align_bytes=64) for h in range(HALVES)]
-               for z in range(PASSES)]
-        u_sc = [[keep.tile([P, P], U8, name="us%d%d" % (z, h), align_bytes=64) for h in range(HALVES)]
-                for z in range(PASSES)]
+        prod1 = [keep.tile([P, J], F32, name="prod1%d" % t) for t in range(PACK)]
+        gf_last = keep.tile([P, P], F32, name="gf_last")
+        grouped0 = keep.tile([P, J, PACK], BF16, name="grouped0", align_bytes=64)
+        grouped1 = [keep.tile([P, P, PACK], BF16, name="grouped1%d" % h, align_bytes=64) for h in range(HALVES)]
+        u_w = [keep.tile([P, J], U32, name="uw%d" % z, align_bytes=64) for z in range(PASSES)]
+        u_sc = [keep.tile([P, J], U8, name="us%d" % z, align_bytes=64) for z in range(PASSES)]
+        halves = [slice(h * P, (h + 1) * P) for h in range(HALVES)]
 
         def load_xb(z):
             rows = xb[z * K_PASS:(z + 1) * K_PASS, :]
             nc.sync.dma_start(xb_t[z][:], rows.rearrange("(p t) s -> p (t s)", t=PACK))
 
-        def load_xf(z, t):
-            rows = xf[z * K_PASS:(z + 1) * K_PASS, :]
-            nc.sync.dma_start(xf_t[z][t][:], rows.rearrange("(p t) c -> p t c", t=PACK)[:, t, :])
-
         load_xb(0)
         nc.sync.dma_start(offs2_t[:], offs2)
         nc.sync.dma_start(offs_t[:], offs)
-        nc.scalar.dma_start(bi_col[:], bi.rearrange("o (p c) -> p (o c)", c=2))
         nc.scalar.dma_start(fk_t[:], fk.rearrange("(z p t) o -> p z (t o)", z=PASSES, t=PACK))
+        nc.scalar.dma_start(bi_col[:], bi.rearrange("o (p c) -> p (o c)", c=2))
         make_identity(nc, ident[:])
         nc.gpsimd.memset(ky_sc[:].bitcast(I32), 0)
-        for q in range(4):
-            nc.gpsimd.dma_start(ky_sc[32 * q:32 * q + 4, :, :].bitcast(I32),
-                                ky_scales[:, 4 * q:4 * q + 4, :].rearrange("z r c -> r z c").bitcast(I32))
-        load_xf(0, PLANE_ORDER[0])
-        load_xf(0, PLANE_ORDER[1])
+        nc.sync.dma_start(xf0[:], xf[0:K_PASS, :].rearrange("(p t) c -> p (t c)", t=PACK))
         load_xb(1)
-        load_xf(0, PLANE_ORDER[2])
-        load_xf(0, PLANE_ORDER[3])
-        for t in PLANE_ORDER:
-            load_xf(1, t)
+        for t in range(PACK):
+            nc.sync.dma_start(xf1[t][:], xf[K_PASS:K, :].rearrange("(p t) c -> p t c", t=PACK)[:, t, :])
+        for q in range(4):
+            nc.sync.dma_start(ky_sc[32 * q:32 * q + 4, :, :].bitcast(I32),
+                              ky_scales[:, 4 * q:4 * q + 4, :].rearrange("z r c -> r z c").bitcast(I32))
         for z in range(PASSES):
             nc.sync.dma_start(ky_w[z][:].bitcast(I32), ky_words[z].rearrange("p c r -> p (c r)").bitcast(I32))
 
         def gather_xb(z, t):
             nc.scalar.activation(gb[z][t][:], xb_t[z][:, t * S:(t + 1) * S].indirect(offs2_t[:]), ACT.Copy)
 
-        def product(z, t, h=None):
-            if h is None:
-                nc.vector.tensor_tensor(prod[z][t][:], xf_t[z][t][:].indirect(offs_t[:]), gb[z][t][:], ALU.mult)
-            else:
-                cols = slice(h * P, (h + 1) * P)
-                nc.vector.tensor_tensor(prod[z][t][:, cols], xf_t[z][t][:].indirect(offs_t[:, 8 * h:8 * h + 8]),
-                                        gb[z][t][:, cols], ALU.mult)
+        def round_on_vector(dst, src, z, t):
+            nc.vector.tensor_scalar(dst[:, :, t], src, fk_t[:, z, t:t + 1], None, ALU.mult)
 
-        def round_into(z, t):
-            for h in range(HALVES):
-                src = prod[z][t][:, h * P:(h + 1) * P]
-                if t < 2:
-                    nc.scalar.activation(grouped[z][h][:, :, t], src, ACT.Copy, scale=fk_t[:, z, t:t + 1])
-                else:
-                    nc.vector.tensor_scalar(grouped[z][h][:, :, t], src, fk_t[:, z, t:t + 1], None, ALU.mult)
+        def round_on_scalar(dst, src, z, t):
+            nc.scalar.activation(dst[:, :, t], src, ACT.Copy, scale=fk_t[:, z, t:t + 1])
 
-        def quantize(z):
-            for h in range(HALVES):
-                nc.vector.quantize_mx(out=u_w[z][h][:].bitcast(E5M2X4), scales=u_sc[z][h][:],
-                                      in_=grouped[z][h][:].rearrange("p j t -> p (j t)"))
+        def quantize(z, cols, src):
+            nc.vector.quantize_mx(out=u_w[z][:, cols].bitcast(E5M2X4), scales=u_sc[z][:, cols],
+                                  in_=src[:].rearrange("p j t -> p (j t)"))
 
+        for t in range(PACK):
+            gather_xb(0, t)
         spread = psum.tile([P, 2, P], F32, name="spread")
         for c in range(2):
             nc.tensor.transpose(spread[:, c, :], bi_col[:, c:c + 1].to_broadcast([P, P]), ident[:])
         nc.scalar.activation(bias[:].rearrange("p (n c) -> p n c", c=2), spread[:].rearrange("p c n -> p n c"),
                              ACT.Copy)
-        for t in PLANE_ORDER:
-            gather_xb(0, t)
-
-        for t in PLANE_ORDER[:2]:
-            product(0, t)
-            round_into(0, t)
-        for t in PLANE_ORDER:
+        for t in range(PACK):
+            window = xf0[:, t * T:(t + 1) * T].indirect(offs_t[:])
+            if t < 2:
+                nc.vector.tensor_copy(gf0[t][:], window)
+            else:
+                nc.scalar.activation(gf0[t][:], window, ACT.Copy)
+        for t in range(PACK):
             gather_xb(1, t)
-        for t in PLANE_ORDER[2:]:
-            product(0, t)
-            round_into(0, t)
-        quantize(0)
-        for t in PLANE_ORDER[:3]:
-            product(1, t)
-            round_into(1, t)
-        for h in range(HALVES):
-            product(1, PLANE_ORDER[3], h)
-        round_into(1, PLANE_ORDER[3])
-        quantize(1)
+        for t in range(PACK):
+            nc.vector.scalar_tensor_tensor(prod0[:, t, :], gf0[t][:], fk_t[:, 0, t:t + 1], gb[0][t][:],
+                                           ALU.mult, ALU.mult)
+        nc.vector.tensor_copy(grouped0[:], prod0[:].rearrange("p t j -> p j t"))
+        quantize(0, slice(0, J), grouped0)
+        for t in range(PACK - 1):
+            nc.vector.tensor_tensor(prod1[t][:], xf1[t][:].indirect(offs_t[:]), gb[1][t][:], ALU.mult)
+            for h in range(HALVES):
+                if t < 2:
+                    round_on_scalar(grouped1[h], prod1[t][:, halves[h]], 1, t)
+                else:
+                    round_on_vector(grouped1[h], prod1[t][:, halves[h]], 1, t)
+        t = PACK - 1
+        nc.scalar.activation(gf_last[:], xf1[t][:].indirect(offs_t[:, 8:16]), ACT.Copy)
+        nc.vector.tensor_tensor(prod1[t][:, halves[0]], xf1[t][:].indirect(offs_t[:, 0:8]),
+                                gb[1][t][:, halves[0]], ALU.mult)
+        round_on_scalar(grouped1[0], prod1[t][:, halves[0]], 1, t)
+        nc.vector.scalar_tensor_tensor(grouped1[1][:, :, t], gf_last[:], fk_t[:, 1, t:t + 1],
+                                       gb[1][t][:, halves[1]], ALU.mult, ALU.mult)
+        quantize(1, halves[1], grouped1[1])
+        quantize(1, halves[0], grouped1[0])
 
         acc = [psum.tile([P, I], F32, name="acc%d" % h) for h in range(HALVES)]
         for z in range(PASSES):
-            for h in range(HALVES):
-                nc.tensor.matmul_mx(out=acc[h][:], lhsT=u_w[z][h][:].bitcast(E5M2X4), lhsT_scale=u_sc[z][h][:],
+            for h in (1, 0):
+                nc.tensor.matmul_mx(out=acc[h][:], lhsT=u_w[z][:, halves[h]].bitcast(E5M2X4),
+                                    lhsT_scale=u_sc[z][:, halves[h]],
                                     rhs=ky_w[z][:].bitcast(E4M3X4), rhs_scale=ky_sc[:, z, :],
                                     start=(z == 0), stop=(z == PASSES - 1))
 
@@ -141,18 +138,26 @@ def tile_list_scores_products_given_centred_kernel(tc, xf, xb, fk, ky_words, ky_
         sums = [keep.tile([P, I // BUNDLE], F32, name="sums%d" % h) for h in range(HALVES)]
         cen = [keep.tile([P, I], F32, name="cen%d" % h) for h in range(HALVES)]
         res = [keep.tile([P, I], F32, name="res%d" % h) for h in range(HALVES)]
-        for h in range(HALVES):
+
+        def add_bias(h):
             nc.vector.tensor_tensor(a[h][:], acc[h][:], bias[:], ALU.add)
             nc.scalar.activation(mag[h][:], a[h][:], ACT.Abs)
-        for h in range(HALVES):
+
+        def sum_bundles(h):
             nc.vector.tensor_reduce(sums[h][:], a[h][:].rearrange("p (g e) -> p g e", e=BUNDLE),
                                     mybir.AxisListType.X, ALU.add)
-        for h in range(HALVES):
+
+        def centre(h):
             nc.vector.scalar_tensor_tensor(cen[h][:].rearrange("p (g e) -> p g e", e=BUNDLE),
                                            sums[h][:].unsqueeze(2).to_broadcast([P, I // BUNDLE, BUNDLE]),
                                            -1.0 / BUNDLE,
                                            a[h][:].rearrange("p (g e) -> p g e", e=BUNDLE),
                                            ALU.mult, ALU.add)
-        for h in range(HALVES):
+
+        def finish(h):
             nc.vector.tensor_tensor(res[h][:], cen[h][:], mag[h][:], ALU.mult)
             nc.sync.dma_start(out[h * P:(h + 1) * P, :], res[h][:])
+
+        for step in (add_bias, sum_bundles, centre, finish):
+            for h in (1, 0):
+                step(h)

from contextlib import ExitStack

import concourse.mybir as mybir
from concourse.masks import make_identity

K, T, J, I, S = 1024, 1024, 256, 256, 512
BUNDLE = 8
FLOPS = 2 * K * J * I

F32 = mybir.dt.float32
BF16 = mybir.dt.bfloat16
I32 = mybir.dt.int32
U32 = mybir.dt.uint32
U16 = mybir.dt.uint16
U8 = mybir.dt.uint8
E4M3X4 = mybir.dt.float8_e4m3fn_x4
E5M2X4 = mybir.dt.float8_e5m2_x4
ALU = mybir.AluOpType
ACT = mybir.ActivationFunctionType

P = 128
PACK = 4
K_PASS = P * PACK
PASSES = K // K_PASS
HALVES = J // P
LIST_COLS = J // 16


def tile_list_scores_products_given_centred_kernel(tc, xf, xb, fk, ky_words, ky_scales, bi, offs, offs2, out):
    nc = tc.nc
    with ExitStack() as ctx:
        keep = ctx.enter_context(tc.tile_pool(name="keep", bufs=1))
        psum = ctx.enter_context(tc.psum_pool(name="psum", bufs=1))

        offs_t = keep.tile([P, LIST_COLS], U16, name="offs_t")
        offs2_t = keep.tile([P, LIST_COLS], U16, name="offs2_t")
        fk_t = keep.tile([P, PASSES, PACK], F32, name="fk_t")
        bi_col = keep.tile([P, 2], F32, name="bi_col")
        ident = keep.tile([P, P], F32, name="ident")
        bias = keep.tile([P, I], F32, name="bias")
        ky_sc = keep.tile([P, PASSES, I], U8, name="ky_sc", align_bytes=64)
        ky_w = [keep.tile([P, I], U32, name="ky_w%d" % z, align_bytes=64) for z in range(PASSES)]
        xb_t = [keep.tile([P, PACK * S], F32, name="xb%d" % z) for z in range(PASSES)]
        xf0 = keep.tile([P, PACK * T], F32, name="xf0")
        xf1 = [keep.tile([P, T], F32, name="xf1%d" % t) for t in range(PACK)]
        gf0 = [keep.tile([P, J], F32, name="gf0%d" % t) for t in range(PACK)]
        prod0 = keep.tile([P, PACK, J], F32, name="prod0")
        gb = [[keep.tile([P, J], F32, name="gb%d%d" % (z, t)) for t in range(PACK)] for z in range(PASSES)]
        prod1 = [keep.tile([P, J], F32, name="prod1%d" % t) for t in range(PACK)]
        gf_last = keep.tile([P, P], F32, name="gf_last")
        grouped0 = keep.tile([P, J, PACK], BF16, name="grouped0", align_bytes=64)
        grouped1 = [keep.tile([P, P, PACK], BF16, name="grouped1%d" % h, align_bytes=64) for h in range(HALVES)]
        u_w = [keep.tile([P, J], U32, name="uw%d" % z, align_bytes=64) for z in range(PASSES)]
        u_sc = [keep.tile([P, J], U8, name="us%d" % z, align_bytes=64) for z in range(PASSES)]
        halves = [slice(h * P, (h + 1) * P) for h in range(HALVES)]

        def load_xb(z):
            rows = xb[z * K_PASS:(z + 1) * K_PASS, :]
            nc.sync.dma_start(xb_t[z][:], rows.rearrange("(p t) s -> p (t s)", t=PACK))

        load_xb(0)
        nc.sync.dma_start(offs2_t[:], offs2)
        nc.sync.dma_start(offs_t[:], offs)
        nc.scalar.dma_start(fk_t[:], fk.rearrange("(z p t) o -> p z (t o)", z=PASSES, t=PACK))
        nc.scalar.dma_start(bi_col[:], bi.rearrange("o (p c) -> p (o c)", c=2))
        make_identity(nc, ident[:])
        nc.gpsimd.memset(ky_sc[:].bitcast(I32), 0)
        nc.sync.dma_start(xf0[:], xf[0:K_PASS, :].rearrange("(p t) c -> p (t c)", t=PACK))
        load_xb(1)
        for t in range(PACK):
            nc.sync.dma_start(xf1[t][:], xf[K_PASS:K, :].rearrange("(p t) c -> p t c", t=PACK)[:, t, :])
        for q in range(4):
            nc.sync.dma_start(ky_sc[32 * q:32 * q + 4, :, :].bitcast(I32),
                              ky_scales[:, 4 * q:4 * q + 4, :].rearrange("z r c -> r z c").bitcast(I32))
        for z in range(PASSES):
            nc.sync.dma_start(ky_w[z][:].bitcast(I32), ky_words[z].rearrange("p c r -> p (c r)").bitcast(I32))

        def gather_xb(z, t):
            nc.scalar.activation(gb[z][t][:], xb_t[z][:, t * S:(t + 1) * S].indirect(offs2_t[:]), ACT.Copy)

        def round_on_vector(dst, src, z, t):
            nc.vector.tensor_scalar(dst[:, :, t], src, fk_t[:, z, t:t + 1], None, ALU.mult)

        def round_on_scalar(dst, src, z, t):
            nc.scalar.activation(dst[:, :, t], src, ACT.Copy, scale=fk_t[:, z, t:t + 1])

        def quantize(z, cols, src):
            nc.vector.quantize_mx(out=u_w[z][:, cols].bitcast(E5M2X4), scales=u_sc[z][:, cols],
                                  in_=src[:].rearrange("p j t -> p (j t)"))

        for t in range(PACK):
            gather_xb(0, t)
        spread = psum.tile([P, 2, P], F32, name="spread")
        for c in range(2):
            nc.tensor.transpose(spread[:, c, :], bi_col[:, c:c + 1].to_broadcast([P, P]), ident[:])
        nc.scalar.activation(bias[:].rearrange("p (n c) -> p n c", c=2), spread[:].rearrange("p c n -> p n c"),
                             ACT.Copy)
        for t in range(PACK):
            window = xf0[:, t * T:(t + 1) * T].indirect(offs_t[:])
            if t < 2:
                nc.vector.tensor_copy(gf0[t][:], window)
            else:
                nc.scalar.activation(gf0[t][:], window, ACT.Copy)
        for t in range(PACK):
            gather_xb(1, t)
        for t in range(PACK):
            nc.vector.scalar_tensor_tensor(prod0[:, t, :], gf0[t][:], fk_t[:, 0, t:t + 1], gb[0][t][:],
                                           ALU.mult, ALU.mult)
        nc.vector.tensor_copy(grouped0[:], prod0[:].rearrange("p t j -> p j t"))
        quantize(0, slice(0, J), grouped0)
        for t in range(PACK - 1):
            nc.vector.tensor_tensor(prod1[t][:], xf1[t][:].indirect(offs_t[:]), gb[1][t][:], ALU.mult)
            for h in range(HALVES):
                if t < 2:
                    round_on_scalar(grouped1[h], prod1[t][:, halves[h]], 1, t)
                else:
                    round_on_vector(grouped1[h], prod1[t][:, halves[h]], 1, t)
        t = PACK - 1
        nc.scalar.activation(gf_last[:], xf1[t][:].indirect(offs_t[:, 8:16]), ACT.Copy)
        nc.vector.tensor_tensor(prod1[t][:, halves[0]], xf1[t][:].indirect(offs_t[:, 0:8]),
                                gb[1][t][:, halves[0]], ALU.mult)
        round_on_scalar(grouped1[0], prod1[t][:, halves[0]], 1, t)
        nc.vector.scalar_tensor_tensor(grouped1[1][:, :, t], gf_last[:], fk_t[:, 1, t:t + 1],
                                       gb[1][t][:, halves[1]], ALU.mult, ALU.mult)
        quantize(1, halves[1], grouped1[1])
        quantize(1, halves[0], grouped1[0])

        acc = [psum.tile([P, I], F32, name="acc%d" % h) for h in range(HALVES)]
        for z in range(PASSES):
            for h in (1, 0):
                nc.tensor.matmul_mx(out=acc[h][:], lhsT=u_w[z][:, halves[h]].bitcast(E5M2X4),
                                    lhsT_scale=u_sc[z][:, halves[h]],
                                    rhs=ky_w[z][:].bitcast(E4M3X4), rhs_scale=ky_sc[:, z, :],
                                    start=(z == 0), stop=(z == PASSES - 1))

        a = [keep.tile([P, I], F32, name="a%d" % h) for h in range(HALVES)]
        mag = [keep.tile([P, I], F32, name="mag%d" % h) for h in range(HALVES)]
        sums = [keep.tile([P, I // BUNDLE], F32, name="sums%d" % h) for h in range(HALVES)]
        cen = [keep.tile([P, I], F32, name="cen%d" % h) for h in range(HALVES)]
        res = [keep.tile([P, I], F32, name="res%d" % h) for h in range(HALVES)]

        def add_bias(h):
            nc.vector.tensor_tensor(a[h][:], acc[h][:], bias[:], ALU.add)
            nc.scalar.activation(mag[h][:], a[h][:], ACT.Abs)

        def sum_bundles(h):
            nc.vector.tensor_reduce(sums[h][:], a[h][:].rearrange("p (g e) -> p g e", e=BUNDLE),
                                    mybir.AxisListType.X, ALU.add)

        def centre(h):
            nc.vector.scalar_tensor_tensor(cen[h][:].rearrange("p (g e) -> p g e", e=BUNDLE),
                                           sums[h][:].unsqueeze(2).to_broadcast([P, I // BUNDLE, BUNDLE]),
                                           -1.0 / BUNDLE,
                                           a[h][:].rearrange("p (g e) -> p g e", e=BUNDLE),
                                           ALU.mult, ALU.add)

        def finish(h):
            nc.vector.tensor_tensor(res[h][:], cen[h][:], mag[h][:], ALU.mult)
            nc.sync.dma_start(out[h * P:(h + 1) * P, :], res[h][:])

        for step in (add_bias, sum_bundles, centre, finish):
            for h in (1, 0):
                step(h)
